import numpy as np, ml_dtypes
CORES = [36,164,52,180,100,228,116,244]
N = 8
BF = ml_dtypes.bfloat16
def f(rng, *shape):
    return (rng.standard_normal(shape, dtype=np.float32) * np.exp2(rng.integers(-2, 3, shape[:-1] + (1,)))).astype(BF)
def wide(rng, *shape):
    v = f(rng, *shape).astype(np.float32); k = shape[:-2] + (1, shape[-1])
    return (v * np.exp2(rng.integers(-6, 7, k)) * (rng.random(k) > 0.0625)).astype(BF)
def gentries(a):
    return np.ascontiguousarray(a.reshape(8, 16, -1).transpose(0, 2, 1)).reshape(8, -1)
def gtable(e):
    e = np.asarray(e); return np.ascontiguousarray(e.reshape(8, -1, 16).transpose(0, 2, 1)).reshape(128, -1).astype(np.int32)
W, F, U, CAP, SW = 4, 96, 2, 8, 2
C = W * F; Z = C + (W - 1) * N * CAP
def pack(x):
    return np.stack([gtable(v.reshape(8, -1)) for v in x])
def unpack(x):
    return np.stack([gentries(v) for v in x])
def sends(rng, full):
    x = np.argsort(rng.random((N, 8, W - 1, N, F)), axis=-1)[..., :CAP] + F * np.arange(W - 1).reshape(1, 1, W - 1, 1, 1)
    n = rng.integers(0, CAP + 1, (N, 8, W - 1, N, 1)); n[0, :, 0, 1] = CAP
    if full: n[:] = CAP
    keep = (np.argsort(rng.random(x.shape), axis=-1) < n) & (np.arange(N).reshape(N, 1, 1, 1, 1) != np.arange(N).reshape(1, 1, 1, N, 1))
    return np.where(keep, x, Z)
def upwind(rng, far, none):
    s = (N, 8, W, U, F); r = np.arange(N).reshape(N, 1, 1, 1, 1); w = np.arange(W).reshape(1, 1, W, 1, 1)
    v = np.where(rng.random(s) < 0.75, w - 1, (rng.random(s) * w).astype(np.int64))
    near = v * F + rng.integers(0, F, s); away = C + (v * N + (r + 1 + rng.integers(0, N - 1, s)) % N) * CAP + rng.integers(0, CAP, s)
    p = rng.random(s)
    return np.where(w == 0, Z, np.where(p < far, away, np.where(p < far + none, Z, near)))
def draw(rng, o, p, x):
    return {"qs": f(rng, N, 128, C), "rm": (0.5 + 0.5 * rng.random((N, 128, C))).astype(BF), "co": (0.75 * rng.random((N, 128, U * C))).astype(BF),
            "sc": (f(rng, N, 16, 16).astype(np.float32) * np.float32(0.0625)).astype(BF), "seq": pack(o), "up": pack(p), "snd": pack(x)}
def orders(rng):
    return np.argsort(rng.random((N, 8, C)), axis=-1)
def setup_inputs(rng):
    return draw(rng, orders(rng), upwind(rng, 0.5, 0.1), sends(rng, False))
def setup_inputs_full(rng):
    return draw(rng, orders(rng), upwind(rng, 0.9, 0.0), sends(rng, True))
def setup_inputs_chain(rng):
    w = np.arange(W).reshape(1, 1, W, 1, 1); r = np.arange(N).reshape(N, 1, 1, 1, 1); x = sends(rng, True)
    p = np.where(w == 0, Z, C + ((w - 1) * N + (r + 1) % N) * CAP + rng.integers(0, CAP, (N, 8, W, U, F)))
    other = np.arange(N).reshape(N, 1, 1, 1) != np.arange(N).reshape(1, 1, 1, N); a = F * np.arange(W - 1).reshape(1, 1, W - 1, 1)
    x[..., 0] = np.where(other, a, Z); x[..., CAP - 1] = np.where(other, a + F - 1, Z)
    return draw(rng, orders(rng), p, x)
def setup_inputs_alike(rng):
    x = sends(rng, True); x[:] = x[..., :1].copy(); p = upwind(rng, 0.5, 0.1); p = np.repeat(p[:, :, :, :1], U, axis=3)
    o = orders(rng); o[:, 0] = np.arange(C); o[:, 1] = np.arange(C)[::-1]; o[:, 3] = o[:, 2]
    return draw(rng, o, p, x)
def setup_inputs_few(rng):
    x = sends(rng, False); k = int(rng.integers(0, N)); x[k] = Z; x[:, :, :, k] = Z
    d = draw(rng, orders(rng), upwind(rng, 0.08, 0.85), x); d["rm"] = np.where(rng.random(d["rm"].shape) < 0.125, np.float32(0), d["rm"].astype(np.float32)).astype(BF)
    return d
def setup_inputs_spread(rng):
    d = setup_inputs(rng); d["qs"] = wide(rng, N, 128, C); return d
def check_inputs(d):
    bad = []
    if not (np.sort(unpack(d["seq"]), axis=-1) == np.arange(C)).all(): bad.append("seq")
    p = unpack(d["up"]).reshape(N, 8, W, U * F).astype(np.int64); w = np.arange(W).reshape(1, 1, W, 1); r = np.arange(N).reshape(N, 1, 1, 1); s = p - C
    if not ((p == Z) | ((p >= 0) & (p < w * F)) | ((s >= 0) & (s < w * N * CAP) & ((s // CAP) % N != r))).all(): bad.append("up")
    x = unpack(d["snd"]).reshape(N, 8, W - 1, N, CAP).astype(np.int64); w = np.arange(W - 1).reshape(1, 1, W - 1, 1, 1)
    other = np.arange(N).reshape(N, 1, 1, 1, 1) != np.arange(N).reshape(1, 1, 1, N, 1)
    if not ((x == Z) | ((x >= w * F) & (x < w * F + F) & other)).all(): bad.append("snd")
    if not all(np.isfinite(d[k].astype(np.float32)).all() for k in ("qs", "rm", "co", "sc")): bad.append("finite")
    return bad
def reference(qs, rm, co, sc, seq, up, snd):
    o = unpack(seq).astype(np.int64); p = unpack(up).astype(np.int64); x = unpack(snd).astype(np.int64)
    src = qs.astype(np.float64).reshape(N, 8, 16, C); rem = rm.astype(np.float64).reshape(N, 8, 16, C); a = co.astype(np.float64).reshape(N, 8, 16, W, U, F)
    s = sc.astype(np.float64).transpose(0, 2, 1); y = np.zeros((N, 16, C), np.float64)
    for k in range(SW):
        win = np.zeros((N, 8, 16, Z + 1), np.float64)
        for w in range(W):
            c = o[:, :, None, w * F:w * F + F]
            h = np.take_along_axis(win, p[:, :, None, w * U * F:(w + 1) * U * F], 3).reshape(N, 8, 16, U, F)
            v = (np.take_along_axis(src, c, 3) + np.sum(a[:, :, :, w] * h, axis=3)) * np.take_along_axis(rem, c, 3)
            v = np.maximum(v, 0.0)
            win[..., w * F:w * F + F] = v
            if w == W - 1: continue
            for r in range(N):
                for q in range(N):
                    if q == r: continue
                    b = C + (w * N + r) * CAP; e = (w * N + q) * CAP
                    win[q, :, :, b:b + CAP] = np.take_along_axis(win[r], x[r][:, None, e:e + CAP], 2)
        psi = np.zeros((N, 8, 16, C), np.float64); np.put_along_axis(psi, o[:, :, None], win[..., :C], 3)
        flux = np.sum(psi, axis=1); y = flux
        src = np.repeat(np.matmul(s, flux)[:, None], 8, axis=1)
    return {"y": y.astype(np.float32)}

from concourse.bass import DstId, RemoteDMATransfer
from concourse.mybir import AluOpType, ActivationFunctionType

A = AluOpType
ACT = ActivationFunctionType

NW, F, CAP, SW = 4, 96, 8, 2
C = NW * F
F32, BF16, I32, U16 = "float32", "bfloat16", "int32", "uint16"
ZC = 192
P0 = 200
WINW = P0 + 3 * F


def slot_col(w):
    return 64 * (2 - w)


def _scratch():
    s = {}

    def sb(name, cols, dt=F32):
        s[name] = ("sbuf", [128, cols], dt)
    sb("seqi", 24, I32)
    sb("sndi", 12, I32)
    sb("upi", 36, I32)
    sb("sequ", 24, U16)
    sb("upm", 36, U16)
    sb("comp", 4, U16)
    sb("qsb", C, BF16)
    sb("rmb", C, BF16)
    sb("cob", 576, BF16)
    sb("scb", 16, BF16)
    sb("iof", C)
    sb("ioi", 16, I32)
    sb("anded", 16, I32)
    sb("sel", 16)
    sb("mask", 128)
    sb("nmask", 128)
    sb("scl", 128)
    sb("zero", F)
    sb("qsp", C)
    sb("rmp", C)
    for w in range(3):
        sb("xl%d" % w, 4, U16)
        sb("sp%d" % w, 104)
    sb("sp3", F)
    sb("cop1", 200)
    sb("cop2", 200)
    sb("cop3", 192)
    for w in (1, 2):
        sb("coc%d" % w, 128)
        sb("spc%d" % w, 64)
        sb("upc%d" % w, 8, U16)
        for u in (0, 1):
            sb("uf%d%d" % (w, u), 104)
    sb("sqf", 104)
    for n in ("fa", "fb", "fc", "fd", "fe", "ff", "fg", "fh"):
        sb(n, 36)
    sb("mu", 128)
    sb("scn", 128)
    sb("tc", 128)
    sb("ts1", 64)
    sb("ts2", 64)
    sb("tf", 192)
    sb("pa", F)
    sb("pb", F)
    sb("cell", C)
    sb("sr", C + 8)
    sb("yb", C)
    for k in range(SW):
        sb("win%d" % k, WINW)
    for r in range(3 * SW):
        sb("send%d" % r, 64)
    for c in range(3):
        s["ps%d" % c] = ("psum", [128, 512], F32)
    return s


SCRATCH = _scratch()
SEMAPHORES = ["arr%d" % r for r in range(6)] + ["sent"] + ["s%d" % i for i in range(143)]


def scheduler(g, T):
    queues = {"v": g.vector, "s": g.scalar, "p": g.tensor, "g": g, "y": g.sync}
    known = {q: set() for q in queues}
    ops, wr, rd, total, waited = [], {}, {}, {}, {}
    names = {}

    def sem_of(label):
        if label.startswith("arr"):
            return T.sem[label]
        if label not in names:
            names[label] = "s%d" % len(names)
        return T.sem[names[label]]

    def hits(table, reg):
        n, a, b = reg
        return [i for (x, y, i) in table.get(n, []) if x < b and a < y]

    def record(q, label, inc, R, W, kn):
        i = len(ops)
        ops.append((label, frozenset(kn)))
        total[label] = total.get(label, 0) + inc
        for (n, a, b) in W:
            wr[n] = [e for e in wr.get(n, []) if not (a <= e[0] and e[1] <= b)] + [(a, b, i)]
            rd[n] = [e for e in rd.get(n, []) if not (a <= e[0] and e[1] <= b)]
        for (n, a, b) in R:
            rd.setdefault(n, []).append((a, b, i))
        return i

    def wait(q, deps):
        deps = sorted((d for d in deps if d not in known[q]), key=lambda d: (ops[d][0].startswith("arr"), d))
        deps = [d for d in deps if not any(d in ops[e][1] for e in deps if e != d)]
        done = set()
        for d in deps:
            label = ops[d][0]
            if label not in done:
                done.add(label)
                queues[q].wait_ge(sem_of(label), total[label])
                waited[label] = total[label]
            for j, o in enumerate(ops):
                if o[0] == label:
                    known[q].add(j)
                    known[q] |= o[1]

    def op(q, label, fn, R=(), W=(), inc=1, fresh=False):
        deps = set()
        if not fresh:
            for reg in R:
                deps.update(hits(wr, reg))
            for reg in W:
                deps.update(hits(wr, reg))
                deps.update(hits(rd, reg))
        wait(q, deps)
        inst = fn(queues[q])
        inst.then_inc(sem_of(label), inc)
        record(q, label, inc, R, W, known[q])

    def need(q, R):
        deps = set()
        for reg in R:
            deps.update(hits(wr, reg))
        wait(q, deps)

    def arrival(label, n, reg):
        i = len(ops)
        ops.append((label, frozenset()))
        total[label] = n
        wr.setdefault(reg[0], []).append((reg[1], reg[2], i))

    def finish(q):
        for label in total:
            if waited.get(label, 0) < total[label]:
                queues[q].wait_ge(sem_of(label), total[label])
    return op, need, arrival, finish


def rank_program(g, core, T, topo):
    rank = T.rank_of(core)
    if rank is None:
        return
    N = len(T.cores)
    op, need, arrival, finish = scheduler(g, T)

    def ts(label, out, R, W, in0, s1, op0, s2=None, op1=None):
        if op1 is None:
            op("v", label, lambda e: e.tensor_scalar(out=out, in0=in0, scalar1=s1, scalar2=None, op0=op0), R, W)
        else:
            op("v", label, lambda e: e.tensor_scalar(out=out, in0=in0, scalar1=s1, scalar2=s2, op0=op0, op1=op1), R, W)

    def tt(label, out, R, W, in0, in1, o):
        op("v", label, lambda e: e.tensor_tensor(out=out, in0=in0, in1=in1, op=o), R, W)

    def vcopy(label, out, R, W, in_):
        op("v", label, lambda e: e.tensor_copy(out=out, in_=in_), R, W)

    def scopy(label, out, R, W, in_):
        op("s", label, lambda e: e.activation(out=out, in_=in_, func=ACT.Copy), R, W)

    def fill(label, name, a, b, v):
        op("v", label, lambda e: e.memset(T[name][:, a:b], v), (), [(name, a, b)], fresh=True)

    def load(q, label, name, out, in_, cols):
        op(q, label, lambda e: e.dma_start(out, in_), (), [(name, 0, cols)], inc=16, fresh=True)

    def send(r, k, w):
        buf, win = "send%d" % r, "win%d" % k
        need("g", [(buf, 0, 64)])
        col = slot_col(w) + CAP * rank
        tr = []
        for i in range(N - 1):
            d = (rank + 1 + i) % N
            dst = T.cores[d]
            rid, pid = topo.addr(dst, core)
            eng = topo.engines(core, dst)
            tr.append(RemoteDMATransfer(dst_ids=[DstId(rid=rid, pnc=pid)], dma_engine_mask=1 << eng[i % len(eng)],
                                        remote_sem=T.sem["arr%d" % r], src=T[buf][:, CAP * d:CAP * d + CAP],
                                        dst=T[win][:, col:col + CAP]))
        g.remote_dma_fused(tr, local_sem=T.sem["sent"])

    def seq(w, n=1):
        return T["sequ"][:, 6 * w:6 * (w + n)]

    load("y", "l_seq", "seqi", T["seqi"][:], T.seq[:], 24)
    load("s", "l_qs", "qsb", T["qsb"][:], T.qs[:], C)
    load("s", "l_rm", "rmb", T["rmb"][:], T.rm[:], C)
    load("y", "l_snd", "sndi", T["sndi"][:], T.snd[:], 12)
    load("y", "l_up", "upi", T["upi"][:], T.up[:, 12:48], 36)
    load("s", "l_co", "cob", T["cob"][:], T.co[:, 192:768], 576)
    for q in range(8):
        load("y", "l_sc", "scb", T["scb"][16 * q:16 * q + 16, :], T.sc[:], 16)

    op("g", "ioi", lambda e: e.iota(T["ioi"][:], [[1, 16]], 128, -1), (), [("ioi", 0, 16)])
    op("g", "iof", lambda e: e.iota(T["iof"][:], [[1, C]], 0, 0, allow_small_or_imprecise_dtypes=True), (), [("iof", 0, C)])
    fill("fills", "sp0", 96, 104, 0.0)
    for k in range(SW):
        fill("fills", "win%d" % k, ZC, ZC + 8, 0.0)
        for w in range(3):
            a = slot_col(w) + CAP * rank
            fill("fills", "win%d" % k, a, a + CAP, 0.0)
    ts("anded", T["anded"][:], [("ioi", 0, 16)], [("anded", 0, 16)], T["ioi"][:], 15, A.bitwise_and)
    ts("sel", T["sel"][:], [("anded", 0, 16)], [("sel", 0, 16)], T["anded"][:], 0, A.is_equal)
    for w in (1, 2):
        fill("fills", "sp%d" % w, 96, 104, 0.0)
        fill("fills", "cop%d" % w, 192, 200, 0.0)
        for u in (0, 1):
            fill("fills", "uf%d%d" % (w, u), 96, 104, float(64 * w))
    fill("fills", "sr", C, C + 8, 0.0)
    fill("fills", "sqf", 96, 104, float(C))
    fill("fills", "zero", 0, F, 0.0)
    for r in range(3 * SW):
        a = slot_col(r % 3)
        arrival("arr%d" % r, N - 1, ("win%d" % (r // 3), a, a + 64))
    scopy("mk0", T["mask"][:, 0:16], [("sel", 0, 16)], [("mask", 0, 16)], T["sel"][:])
    n = 16
    while n < 128:
        scopy("mk%d" % n, T["mask"][:, n:2 * n], [("mask", 0, n)], [("mask", n, 2 * n)], T["mask"][:, 0:n])
        n *= 2
    op("s", "nmask", lambda e: e.activation(out=T["nmask"][:], in_=T["mask"][:], func=ACT.Identity, bias=1.0, scale=-1.0),
       [("mask", 0, 128)], [("nmask", 0, 128)])

    def local_list(w):
        ts("xl%d" % w, T["xl%d" % w][:], [("sndi", 0, 12)], [("xl%d" % w, 0, 4)], T["sndi"][:, 4 * w:4 * w + 4],
           float(F * w), A.subtract, float(F), A.min)

    def xl(w):
        return T["xl%d" % w][:, 0:4]

    vcopy("sequ", T["sequ"][:], [("seqi", 0, 24)], [("sequ", 0, 24)], T["seqi"][:])
    local_list(0)
    vcopy("qsp0", T["qsp"][:, 0:F], [("qsb", 0, C), ("sequ", 0, 24)], [("qsp", 0, F)], T["qsb"][:, 0:C].indirect(seq(0)))
    tt("sp0", T["sp0"][:, 0:F], [("rmb", 0, C), ("sequ", 0, 24), ("qsp", 0, F)], [("sp0", 0, F)],
       T["rmb"][:, 0:C].indirect(seq(0)), T["qsp"][:, 0:F], A.mult)
    ts("send0", T["send0"][:], [("sp0", 0, 104), ("xl0", 0, 4)], [("send0", 0, 64)],
       T["sp0"][:, 0:104].indirect(xl(0)), 0.0, A.max)
    send(0, 0, 0)

    for (a, n) in ((1, 1), (2, 2)):
        for (name, src) in (("rmp", "rmb"), ("qsp", "qsb")):
            scopy("%s%d" % (name, a), T[name][:, F * a:F * (a + n)], [(src, 0, C), ("sequ", 0, 24)],
                  [(name, F * a, F * (a + n))], T[src][:, 0:C].indirect(seq(a, n)))

    def psi_cols(w):
        return P0 + F * w, P0 + F * w + F

    def scatter(k, w, label):
        a, b = psi_cols(w)
        vcopy(label, T["cell"][:, 0:C].indirect(seq(w)), [("win%d" % k, a, b), ("sequ", 0, 24)], [("cell", 0, C)],
              T["win%d" % k][:, a:b])

    a0, b0 = psi_cols(0)
    ts("psi00", T["win0"][:, a0:b0], [("sp0", 0, F)], [("win0", a0, b0)], T["sp0"][:, 0:F], 0.0, A.max)

    def remap1():
        ts("fb", T["fb"][:], [("upi", 0, 36)], [("fb", 0, 36)], T["upi"][:], 384.0, A.is_ge, -456.0, A.mult)
        ts("fa1", T["fa"][:, 0:12], [("upi", 0, 36)], [("fa", 0, 12)], T["upi"][:, 0:12], 448.0, A.min, 72.0, A.add)
        tt("fc", T["fc"][:, 0:12], [("fa", 0, 12), ("fb", 0, 12)], [("fc", 0, 12)], T["fa"][:, 0:12], T["fb"][:, 0:12], A.add)
        vcopy("upm1", T["upm"][:, 0:12], [("fc", 0, 12)], [("upm", 0, 12)], T["fc"][:, 0:12])

    def remap2():
        for w in (2, 3):
            a, b = 12 * (w - 1), 12 * w
            ts("fa%d" % w, T["fa"][:, a:b], [("upi", 0, 36)], [("fa", a, b)], T["upi"][:, a:b], float(8 + 64 * w), A.add)
        ts("fd", T["fd"][:, 12:36], [("upi", 0, 36)], [("fd", 12, 36)], T["upi"][:, 12:36], 448.0, A.is_ge, -128.0, A.mult)
        tt("fc2", T["fc"][:, 12:36], [("fa", 12, 36), ("fb", 12, 36)], [("fc", 12, 36)], T["fa"][:, 12:36], T["fb"][:, 12:36], A.add)
        tt("fh", T["fh"][:, 12:36], [("fc", 12, 36), ("fd", 12, 36)], [("fh", 12, 36)], T["fc"][:, 12:36], T["fd"][:, 12:36], A.add)
        vcopy("upm2", T["upm"][:, 12:24], [("fh", 12, 24)], [("upm", 12, 24)], T["fh"][:, 12:24])

    def remap3():
        ts("fe", T["fe"][:, 24:36], [("upi", 0, 36)], [("fe", 24, 36)], T["upi"][:, 24:36], 512.0, A.is_ge, -128.0, A.mult)
        ts("ff", T["ff"][:, 24:36], [("upi", 0, 36)], [("ff", 24, 36)], T["upi"][:, 24:36], 576.0, A.is_ge, 128.0, A.mult)
        tt("fg", T["fg"][:, 24:36], [("fe", 24, 36), ("ff", 24, 36)], [("fg", 24, 36)], T["fe"][:, 24:36], T["ff"][:, 24:36], A.add)
        tt("fa4", T["fa"][:, 24:36], [("fh", 24, 36), ("fg", 24, 36)], [("fa", 24, 36)], T["fh"][:, 24:36], T["fg"][:, 24:36], A.add)
        vcopy("upm3", T["upm"][:, 24:36], [("fa", 24, 36)], [("upm", 24, 36)], T["fa"][:, 24:36])

    def products(w):
        rm = T["rmp"][:, F * w:F * w + F]
        sp, cop = "sp%d" % w, "cop%d" % w
        tt(sp, T[sp][:, 0:F], [("rmp", F * w, F * w + F), ("qsp", F * w, F * w + F)], [(sp, 0, F)],
           T["qsp"][:, F * w:F * w + F], rm, A.mult)
        for u in (0, 1):
            c = 192 * (w - 1) + F * u
            tt("%s%d" % (cop, u), T[cop][:, F * u:F * u + F], [("cob", 0, 576), ("rmp", F * w, F * w + F)],
               [(cop, F * u, F * u + F)], T["cob"][:, c:c + F], rm, A.mult)

    def flat_up(w):
        for u in (0, 1):
            c, n = 12 * (w - 1) + 6 * u, "uf%d%d" % (w, u)
            scopy(n, T[n][:, 0:F], [("iof", 0, C), ("upm", c, c + 6)], [(n, 0, F)], T["iof"][:, 0:C].indirect(T["upm"][:, c:c + 6]))

    def sent_s(w, tag):
        sp, spc = "sp%d" % w, "spc%d" % w
        scopy(spc + tag, T[spc][:], [(sp, 0, 104), ("xl%d" % w, 0, 4)], [(spc, 0, 64)], T[sp][:, 0:104].indirect(xl(w)))

    def sent_co(w):
        cop, coc = "cop%d" % w, "coc%d" % w
        for u in (0, 1):
            scopy("%s%d" % (coc, u), T[coc][:, 64 * u:64 * u + 64], [(cop, F * u, F * u + 104), ("xl%d" % w, 0, 4)],
                  [(coc, 64 * u, 64 * u + 64)], T[cop][:, F * u:F * u + 104].indirect(xl(w)))

    def sent_up(w):
        for u in (0, 1):
            n = "uf%d%d" % (w, u)
            tt("mu%d%d" % (w, u), T["mu"][:, 64 * u:64 * u + 64], [(n, 0, 104), ("xl%d" % w, 0, 4), ("mask", 0, 64)],
               [("mu", 64 * u, 64 * u + 64)], T[n][:, 0:104].indirect(xl(w)), T["mask"][:, 0:64], A.mult)
        op("v", "scn%d" % w, lambda e: e.tensor_tensor_scan(T["scn"][:], T["nmask"][:], T["mu"][:], 0.0, A.mult, A.add),
           [("nmask", 0, 128), ("mu", 0, 128)], [("scn", 0, 128)])
        vcopy("upc%d" % w, T["upc%d" % w][:], [("scn", 0, 128)], [("upc%d" % w, 0, 8)], T["scn"][:, 15::16])

    remap1()
    local_list(1)
    products(1)
    flat_up(1)
    sent_co(1)
    sent_s(1, "a")
    sent_up(1)
    remap2()
    local_list(2)
    flat_up(2)
    products(2)
    sent_co(2)
    sent_s(2, "a")
    for q in range(8):
        scopy("scl", T["scl"][:, 16 * q:16 * q + 16], [("scb", 0, 16)], [("scl", 16 * q, 16 * q + 16)], T["scb"][:])
    scopy("sqf", T["sqf"][:, 0:F], [("iof", 0, C), ("sequ", 0, 24)], [("sqf", 0, F)], T["iof"][:, 0:C].indirect(seq(0)))

    def sent_cells():
        tt("mu0", T["mu"][:, 0:64], [("sqf", 0, 104), ("xl0", 0, 4), ("mask", 0, 64)], [("mu", 0, 64)],
           T["sqf"][:, 0:104].indirect(xl(0)), T["mask"][:, 0:64], A.mult)
        op("v", "scn0", lambda e: e.tensor_tensor_scan(T["scn"][:, 0:64], T["nmask"][:, 0:64], T["mu"][:, 0:64], 0.0, A.mult, A.add),
           [("nmask", 0, 64), ("mu", 0, 64)], [("scn", 0, 64)])
        vcopy("comp", T["comp"][:], [("scn", 0, 64)], [("comp", 0, 4)], T["scn"][:, 15:64:16])

    def window(k, w):
        a, b = 64 * (3 - w), P0 + F * w
        return T["win%d" % k][:, a:b], ("win%d" % k, a, b)

    def sent_psi(k, w):
        r = 3 * k + w
        win, reg = window(k, w)
        coc, spc, upc, z = "coc%d" % w, "spc%d" % w, "upc%d" % w, "%d%d" % (k, w)
        tt("tc" + z, T["tc"][:], [reg, (upc, 0, 8), (coc, 0, 128)], [("tc", 0, 128)], win.indirect(T[upc][:, 0:8]), T[coc][:], A.mult)
        tt("ta" + z, T["ts1"][:], [("tc", 0, 128)], [("ts1", 0, 64)], T["tc"][:, 0:64], T["tc"][:, 64:128], A.add)
        tt("tb" + z, T["ts2"][:], [("ts1", 0, 64), (spc, 0, 64)], [("ts2", 0, 64)], T["ts1"][:], T[spc][:], A.add)
        ts("send%d" % r, T["send%d" % r][:], [("ts2", 0, 64)], [("send%d" % r, 0, 64)], T["ts2"][:], 0.0, A.max)
        send(r, k, w)

    def all_psi(k, w):
        win, reg = window(k, w)
        c, cop, sp, z = 12 * (w - 1), "cop%d" % w, "sp%d" % w, "%d%d" % (k, w)
        tt("tf" + z, T["tf"][:], [reg, ("upm", c, c + 12), (cop, 0, 192)], [("tf", 0, 192)],
           win.indirect(T["upm"][:, c:c + 12]), T[cop][:, 0:192], A.mult)
        tt("pa" + z, T["pa"][:], [("tf", 0, 192)], [("pa", 0, F)], T["tf"][:, 0:F], T["tf"][:, F:192], A.add)
        tt("pb" + z, T["pb"][:], [("pa", 0, F), (sp, 0, F)], [("pb", 0, F)], T["pa"][:], T[sp][:, 0:F], A.add)
        if w < 3:
            a, b = psi_cols(w)
            ts("psi" + z, T["win%d" % k][:, a:b], [("pb", 0, F)], [("win%d" % k, a, b)], T["pb"][:], 0.0, A.max)
        else:
            tt("sc" + z, T["cell"][:, 0:C].indirect(seq(3)), [("pb", 0, F), ("zero", 0, F), ("sequ", 0, 24)], [("cell", 0, C)],
               T["pb"][:], T["zero"][:], A.max)

    for k in range(SW):
        if k:
            for c in range(3):
                a, b, ps = 128 * c, 128 * c + 128, "ps%d" % c
                op("p", "mm%d" % c, lambda e: e.matmul(T[ps][:, 0:128], T["scl"][:], T["cell"][:, a:b], True, True),
                   [("scl", 0, 128), ("cell", a, b)], [(ps, 0, 512)])
            for c in range(3):
                a, b, ps = 128 * c, 128 * c + 128, "ps%d" % c
                tt("sr%d" % c, T["sr"][:, a:b], [(ps, 0, 512), ("rmb", 0, C)], [("sr", a, b)], T[ps][:, 0:128], T["rmb"][:, a:b], A.mult)
            ts("send3", T["send3"][:], [("sr", 0, C + 8), ("comp", 0, 4)], [("send3", 0, 64)],
               T["sr"][:, 0:C + 8].indirect(T["comp"][:, 0:4]), 0.0, A.max)
            send(3, k, 0)
            ts("psi10", T["win1"][:, a0:b0], [("sr", 0, C), ("sequ", 0, 24)], [("win1", a0, b0)],
               T["sr"][:, 0:C].indirect(seq(0)), 0.0, A.max)
            for w in (1, 2, 3):
                sp = "sp%d" % w
                scopy(sp + "b", T[sp][:, 0:F], [("sr", 0, C), ("sequ", 0, 24)], [(sp, 0, F)], T["sr"][:, 0:C].indirect(seq(w)))
                if w < 3:
                    sent_s(w, "b")
            scatter(1, 0, "sc10")
        sent_psi(k, 1)
        all_psi(k, 1)
        if k == 0:
            sent_up(2)
            scatter(0, 0, "sc00")
        scatter(k, 1, "sc%d1" % k)
        sent_psi(k, 2)
        all_psi(k, 2)
        if k == 0:
            remap3()
            products(3)
            sent_cells()
        scatter(k, 2, "sc%d2" % k)
        all_psi(k, 3)

    for c in range(3):
        a, b, ps = 128 * c, 128 * c + 128, "ps%d" % c
        op("p", "my%d" % c, lambda e: e.matmul(T[ps][0:16, 0:128], T["sel"][:], T["cell"][:, a:b], True, True),
           [("sel", 0, 16), ("cell", a, b)], [(ps, 0, 512)])
    for c in range(3):
        a, b, ps = 128 * c, 128 * c + 128, "ps%d" % c
        vcopy("yb%d" % c, T["yb"][0:16, a:b], [(ps, 0, 512)], [("yb", a, b)], T[ps][0:16, 0:128])
    op("y", "l_y", lambda e: e.dma_start(T.y[:], T["yb"][0:16, :]), [("yb", 0, C)], [("y", 0, C)], inc=16)
    g.wait_ge(T.sem["sent"], 3 * SW * (N - 1))
    finish("y")
